import numpy as np, ml_dtypes
CORES = [2,6,26,30,66,70,74,78,82,86]
N = 10
C = 256
def setup_inputs(rng):
    u = np.triu(np.ones((128, 128), np.float32)).astype(ml_dtypes.bfloat16)
    return {"x": rng.standard_normal((N, 128, C), dtype=np.float32).astype(ml_dtypes.bfloat16), "u": np.broadcast_to(u, (N, 128, 128)).copy()}
def setup_inputs_big(rng):
    d = setup_inputs(rng)
    for k in ("x",): d[k] = (d[k].astype(np.float32) * 1048576.0).astype(d[k].dtype)
    return d
def setup_inputs_small(rng):
    d = setup_inputs(rng)
    for k in ("x",): d[k] = (d[k].astype(np.float32) * (1 / 1048576.0)).astype(d[k].dtype)
    return d
def setup_inputs_apart(rng):
    d = setup_inputs(rng)
    f = (10.0 ** rng.permutation(np.linspace(-1.5, 1.5, N))).astype(np.float32).reshape(N, 1, 1)
    for k in ("x",): d[k] = (d[k].astype(np.float32) * f).astype(d[k].dtype)
    return d
def reference(x, u):
    X, U = x.astype(np.float64), u.astype(np.float64)
    y = np.zeros((N, 128, C)); c = np.zeros(C)
    for r in range(N):
        y[r] = U[r].T @ X[r] + c
        c = c + X[r].sum(axis=0)
    return {"y": y.astype(ml_dtypes.bfloat16 if x.dtype != np.float64 else np.float64)}

@@ -1,0 +1,82 @@
+from concourse.bass import DstId, RemoteDMATransfer
+
+N = 10
+ROWS = 128
+C = 256
+P = 8
+E = 4
+SLOTS = ROWS // P
+
+SCRATCH = {
+    "xs": ("dram", [SLOTS, 128, C * P // 128], "bfloat16"),
+    "d": ("dram", [N - 1, 128, C * P // 128], "bfloat16"),
+    "x_sb": ("sbuf", [128, C], "bfloat16"),
+    "u_sb": ("sbuf", [128, 128], "bfloat16"),
+    "ones": ("sbuf", [128, 128], "bfloat16"),
+    "car": ("sbuf", [128, C], "bfloat16"),
+    "y_sb": ("sbuf", [128, C], "bfloat16"),
+    "acc": ("psum", [128, 512], "float32"),
+}
+SEMAPHORES = ["xs_in", "x_in", "u_in", "fill", "sent", "arrived", "car_in", "mm", "cp", "stored"]
+
+
+def _engines(topo, core, dsts, n):
+    common = topo.mask(core, dsts[0])
+    for d in dsts[1:]:
+        common &= topo.mask(core, d)
+    bits = [b for b in range(common.bit_length()) if (common >> b) & 1]
+    m = 0
+    for b in bits[::len(bits) // n][:n]:
+        m |= 1 << b
+    return m
+
+
+def rank_program(g, core, T, topo):
+    r = T.rank_of(core)
+    if r is None:
+        return
+    S = T.sem
+    later = [c for c in T.cores[r + 1:]]
+    k = P * r
+
+    if later:
+        g.sync.dma_start(T.xs[:], T.x[:]).then_inc(S.xs_in, 16)
+    g.scalar.dma_start(T.x_sb[:], T.x[:]).then_inc(S.x_in, 16)
+    g.sync.dma_start(T.u_sb[:], T.u[:]).then_inc(S.u_in, 16)
+    if r:
+        g.vector.memset(T.ones[0:k, :], 1.0).then_inc(S.fill, 1)
+
+    if later:
+        for c in later:
+            assert topo.may_write(core, c)
+        here = topo.chip(core)
+        order = sorted(later, key=lambda c: (topo.chip(c) == here,
+                                             topo.mates(here, topo.chip(c)) or topo.same_plane(here, topo.chip(c))))
+        ids = []
+        for c in order:
+            rid, pid, _ = topo.addr(c)
+            ids.append(DstId(rid=rid, pnc=pid))
+        g.wait_ge(S.xs_in, 16)
+        g.remote_dma_fused([RemoteDMATransfer(dst_ids=ids, dma_engine_mask=_engines(topo, core, order, E),
+                                              remote_sem=S.arrived, srcs=[T.xs[j] for j in range(SLOTS)],
+                                              dsts=[T.d[r] for _ in order], alu_op=1)], local_sem=S.sent)
+
+    g.tensor.wait_ge(S.x_in, 16)
+    g.tensor.wait_ge(S.u_in, 16)
+    first = g.tensor.matmul(T.acc[:, 0:C], T.u_sb[:], T.x_sb[:], True, r == 0)
+    if r == 0:
+        first.then_inc(S.mm, 1)
+    else:
+        g.sync.wait_ge(S.arrived, E * r)
+        g.sync.dma_start(T.car[0:k, :], T.d[0:r]).then_inc(S.car_in, 16)
+        g.tensor.wait_ge(S.fill, 1)
+        g.tensor.wait_ge(S.car_in, 16)
+        g.tensor.matmul(T.acc[:, 0:C], T.ones[0:k, :], T.car[0:k, :], False, True).then_inc(S.mm, 1)
+
+    g.vector.wait_ge(S.mm, 1)
+    g.vector.tensor_copy(T.y_sb[:], T.acc[:, 0:C]).then_inc(S.cp, 1)
+    g.sync.wait_ge(S.cp, 1)
+    g.sync.dma_start(T.y[:], T.y_sb[:]).then_inc(S.stored, 16)
+    g.sync.wait_ge(S.stored, 16)
+    if later:
+        g.wait_ge(S.sent, E)

@@ -3,8 +3,9 @@ from concourse.bass import DstId, RemoteDMATransfer
 N = 10
 ROWS = 128
 C = 256
+H = C // 2
 P = 8
-E = 4
+E = 8
 SLOTS = ROWS // P
 
 SCRATCH = {
@@ -15,9 +16,10 @@ SCRATCH = {
     "ones": ("sbuf", [128, 128], "bfloat16"),
     "car": ("sbuf", [128, C], "bfloat16"),
     "y_sb": ("sbuf", [128, C], "bfloat16"),
-    "acc": ("psum", [128, 512], "float32"),
+    "acc0": ("psum", [128, 512], "float32"),
+    "acc1": ("psum", [128, 512], "float32"),
 }
-SEMAPHORES = ["xs_in", "x_in", "u_in", "fill", "sent", "arrived", "car_in", "mm", "cp", "stored"]
+SEMAPHORES = ["xs_in", "x_in", "u_in", "fill", "sent", "arrived", "car_in", "mm0", "mm1", "cp", "stored"]
 
 
 def _engines(topo, core, dsts, n):
@@ -38,6 +40,8 @@ def rank_program(g, core, T, topo):
     S = T.sem
     later = [c for c in T.cores[r + 1:]]
     k = P * r
+    acc = [T.acc0, T.acc1]
+    done = [S.mm0, S.mm1]
 
     if later:
         g.sync.dma_start(T.xs[:], T.x[:]).then_inc(S.xs_in, 16)
@@ -51,7 +55,8 @@ def rank_program(g, core, T, topo):
             assert topo.may_write(core, c)
         here = topo.chip(core)
         order = sorted(later, key=lambda c: (topo.chip(c) == here,
-                                             topo.mates(here, topo.chip(c)) or topo.same_plane(here, topo.chip(c))))
+                                             topo.mates(here, topo.chip(c)) or topo.same_plane(here, topo.chip(c)),
+                                             -T.rank_of(c)))
         ids = []
         for c in order:
             rid, pid, _ = topo.addr(c)
@@ -63,19 +68,22 @@ def rank_program(g, core, T, topo):
 
     g.tensor.wait_ge(S.x_in, 16)
     g.tensor.wait_ge(S.u_in, 16)
-    first = g.tensor.matmul(T.acc[:, 0:C], T.u_sb[:], T.x_sb[:], True, r == 0)
-    if r == 0:
-        first.then_inc(S.mm, 1)
-    else:
+    for h in range(2):
+        own = g.tensor.matmul(acc[h][:, 0:H], T.u_sb[:], T.x_sb[:, h * H:(h + 1) * H], True, r == 0)
+        if r == 0:
+            own.then_inc(done[h], 1)
+    if r:
         g.sync.wait_ge(S.arrived, E * r)
         g.sync.dma_start(T.car[0:k, :], T.d[0:r]).then_inc(S.car_in, 16)
         g.tensor.wait_ge(S.fill, 1)
         g.tensor.wait_ge(S.car_in, 16)
-        g.tensor.matmul(T.acc[:, 0:C], T.ones[0:k, :], T.car[0:k, :], False, True).then_inc(S.mm, 1)
+        for h in range(2):
+            g.tensor.matmul(acc[h][:, 0:H], T.ones[0:k, :], T.car[0:k, h * H:(h + 1) * H], False, True).then_inc(done[h], 1)
 
-    g.vector.wait_ge(S.mm, 1)
-    g.vector.tensor_copy(T.y_sb[:], T.acc[:, 0:C]).then_inc(S.cp, 1)
-    g.sync.wait_ge(S.cp, 1)
+    for h in range(2):
+        g.vector.wait_ge(done[h], 1)
+        g.vector.tensor_copy(T.y_sb[:, h * H:(h + 1) * H], acc[h][:, 0:H]).then_inc(S.cp, 1)
+    g.sync.wait_ge(S.cp, 2)
     g.sync.dma_start(T.y[:], T.y_sb[:]).then_inc(S.stored, 16)
     g.sync.wait_ge(S.stored, 16)
     if later:

from concourse.bass import DstId, RemoteDMATransfer

N = 10
ROWS = 128
C = 256
H = C // 2
P = 8
E = 8
SLOTS = ROWS // P

SCRATCH = {
    "xs": ("dram", [SLOTS, 128, C * P // 128], "bfloat16"),
    "d": ("dram", [N - 1, 128, C * P // 128], "bfloat16"),
    "x_sb": ("sbuf", [128, C], "bfloat16"),
    "u_sb": ("sbuf", [128, 128], "bfloat16"),
    "ones": ("sbuf", [128, 128], "bfloat16"),
    "car": ("sbuf", [128, C], "bfloat16"),
    "y_sb": ("sbuf", [128, C], "bfloat16"),
    "acc0": ("psum", [128, 512], "float32"),
    "acc1": ("psum", [128, 512], "float32"),
}
SEMAPHORES = ["xs_in", "x_in", "u_in", "fill", "sent", "arrived", "car_in", "mm0", "mm1", "cp", "stored"]


def _engines(topo, core, dsts, n):
    common = topo.mask(core, dsts[0])
    for d in dsts[1:]:
        common &= topo.mask(core, d)
    bits = [b for b in range(common.bit_length()) if (common >> b) & 1]
    m = 0
    for b in bits[::len(bits) // n][:n]:
        m |= 1 << b
    return m


def rank_program(g, core, T, topo):
    r = T.rank_of(core)
    if r is None:
        return
    S = T.sem
    later = [c for c in T.cores[r + 1:]]
    k = P * r
    acc = [T.acc0, T.acc1]
    done = [S.mm0, S.mm1]

    if later:
        g.sync.dma_start(T.xs[:], T.x[:]).then_inc(S.xs_in, 16)
    g.scalar.dma_start(T.x_sb[:], T.x[:]).then_inc(S.x_in, 16)
    g.sync.dma_start(T.u_sb[:], T.u[:]).then_inc(S.u_in, 16)
    if r:
        g.vector.memset(T.ones[0:k, :], 1.0).then_inc(S.fill, 1)

    if later:
        for c in later:
            assert topo.may_write(core, c)
        here = topo.chip(core)
        order = sorted(later, key=lambda c: (topo.chip(c) == here,
                                             topo.mates(here, topo.chip(c)) or topo.same_plane(here, topo.chip(c)),
                                             -T.rank_of(c)))
        ids = []
        for c in order:
            rid, pid, _ = topo.addr(c)
            ids.append(DstId(rid=rid, pnc=pid))
        g.wait_ge(S.xs_in, 16)
        g.remote_dma_fused([RemoteDMATransfer(dst_ids=ids, dma_engine_mask=_engines(topo, core, order, E),
                                              remote_sem=S.arrived, srcs=[T.xs[j] for j in range(SLOTS)],
                                              dsts=[T.d[r] for _ in order], alu_op=1)], local_sem=S.sent)

    g.tensor.wait_ge(S.x_in, 16)
    g.tensor.wait_ge(S.u_in, 16)
    for h in range(2):
        own = g.tensor.matmul(acc[h][:, 0:H], T.u_sb[:], T.x_sb[:, h * H:(h + 1) * H], True, r == 0)
        if r == 0:
            own.then_inc(done[h], 1)
    if r:
        g.sync.wait_ge(S.arrived, E * r)
        g.sync.dma_start(T.car[0:k, :], T.d[0:r]).then_inc(S.car_in, 16)
        g.tensor.wait_ge(S.fill, 1)
        g.tensor.wait_ge(S.car_in, 16)
        for h in range(2):
            g.tensor.matmul(acc[h][:, 0:H], T.ones[0:k, :], T.car[0:k, h * H:(h + 1) * H], False, True).then_inc(done[h], 1)

    for h in range(2):
        g.vector.wait_ge(done[h], 1)
        g.vector.tensor_copy(T.y_sb[:, h * H:(h + 1) * H], acc[h][:, 0:H]).then_inc(S.cp, 1)
    g.sync.wait_ge(S.cp, 2)
    g.sync.dma_start(T.y[:], T.y_sb[:]).then_inc(S.stored, 16)
    g.sync.wait_ge(S.stored, 16)
    if later:
        g.wait_ge(S.sent, E)
